import numpy as np
import ml_dtypes


def mxq(x, axis, fmt="e4m3"):
    dtype, down = {"e4m3": (ml_dtypes.float8_e4m3fn, 7), "e5m2": (ml_dtypes.float8_e5m2, 14)}[fmt]
    v = np.moveaxis(np.asarray(x, np.float32).astype(ml_dtypes.bfloat16).astype(np.float64), axis, -1)
    blocks = v.reshape(v.shape[:-1] + (-1, 32))
    amax = np.abs(blocks).max(-1, keepdims=True)
    byte = np.maximum(np.where(amax > 0, np.frexp(amax)[1] - 1 + 127, 0) - down, 1)
    scale = np.exp2(byte - 127.0)
    codes = (blocks / scale).astype(np.float32).astype(dtype).astype(np.float64)
    return np.moveaxis((codes * scale).reshape(v.shape), -1, axis)


WIDE = False


def mx_kscale(k):
    if not WIDE:
        return np.ones(k)
    levels = np.array([30, -30])
    if k % 512:
        return np.exp2(np.random.permutation(np.resize(levels, k // 32))).repeat(32)
    a = np.empty((k // 512, 16))
    for p in range(k // 512):
        a[p, :8] = np.random.permutation(np.resize(levels, 8))
        for g in range(8):
            far = levels[np.abs(levels - a[p, g]) >= 10]
            a[p, g + 8] = far[np.random.randint(len(far))]
    return np.exp2(a.ravel()).repeat(32)


def f64(x):
    return np.asarray(x).astype(np.float64)


def striped(idx):
    return np.tile(np.asarray(idx).reshape(-1, 16).T, (8, 1)).astype(np.uint16)


def unstriped(offs):
    return offs[:16].T.reshape(-1).astype(np.int64)


E2M1 = np.array([0.0, 0.5, 1.0, 1.5, 2.0, 3.0, 4.0, 6.0, -0.0, -0.5, -1.0, -1.5, -2.0, -3.0, -4.0, -6.0])


def pack_weight(w, fmt):
    k, n = w.shape
    w = f64(np.asarray(w, np.float32).astype(ml_dtypes.bfloat16)).reshape(k // 32, 32, n)
    amax = np.abs(w).max(1)
    if fmt in ("e4m3", "e5m2"):
        byte = np.frexp(amax)[1] - 1 + 127 - (7 if fmt == "e4m3" else 14)
    else:
        mant, ex = np.frexp(amax / 6.0)
        byte = np.where(mant > 0.5, ex, ex - 1) + 127
    byte = np.clip(np.where(amax > 0, byte, 1), 1, 254)
    scaled = (w * np.exp2(127.0 - byte)[:, None, :]).reshape(k, n).astype(np.float32)
    by_word = np.ascontiguousarray(scaled.reshape(k // 512, 128, 4, n).transpose(0, 1, 3, 2))
    if fmt in ("e4m3", "e5m2"):
        words = by_word.astype(ml_dtypes.float8_e4m3fn if fmt == "e4m3" else ml_dtypes.float8_e5m2).view(np.uint8)
    else:
        c = by_word.astype(ml_dtypes.float4_e2m1fn).view(np.uint8) & 0xF
        words = (c[..., 0::2] | (c[..., 1::2] << 4)).reshape(k // 512, 128, 2 * n)
    return np.ascontiguousarray(words), np.ascontiguousarray(byte.astype(np.uint8).reshape(k // 512, 16, n))


def unpack_weight(words, scales, fmt):
    g, _, n = scales.shape
    words = np.ascontiguousarray(words).reshape(g, 128, n, -1)
    if fmt in ("e4m3", "e5m2"):
        vals = words.view(ml_dtypes.float8_e4m3fn if fmt == "e4m3" else ml_dtypes.float8_e5m2).astype(np.float64)
    else:
        nib = np.empty((g, 128, n, 4), np.uint8)
        nib[..., 0::2] = words & 0xF
        nib[..., 1::2] = words >> 4
        vals = E2M1[nib]
    vals = vals * np.repeat(np.exp2(scales.astype(np.float64) - 127.0), 8, axis=1)[..., None]
    return vals.transpose(0, 1, 3, 2).reshape(g * 512, n)


K, T, Z, J, R, C, O, N, L, E = 512, 1024, 1024, 256, 512, 512, 256, 256, 512, 1024


def setup_inputs():
    n = np.random.standard_normal
    idx = np.random.permutation(T)[:J]
    idx2 = np.random.permutation(Z)[:J]
    idx3 = np.random.permutation(C)[:J]
    idx4 = np.random.permutation(C)[:J]
    idx5 = np.random.permutation(C)[:O]
    idx6 = np.random.permutation(C)[:O]
    idx7 = np.random.permutation(E)[:O]
    fk = mx_kscale(K)
    fr = mx_kscale(R)
    fl = mx_kscale(L)
    xtp = pack_weight(n((K, T)) / fk[:, None], "e5m2")
    xop = pack_weight(n((K, Z)) / fk[:, None], "e4m3")
    wp = pack_weight(n((K, R)) * 1 / np.sqrt(K) * fk[:, None] * fr, "e2m1")
    wbp = pack_weight(n((R, N)) * 1 / np.sqrt(R) / fr[:, None], "e2m1")
    sxp = pack_weight(n((L, O)) / fl[:, None], "e4m3")
    wsp = pack_weight(n((L, N)) * 1 / np.sqrt(L) * fl[:, None], "e2m1")
    return {
        "xt_words": xtp[0],
        "xt_scales": xtp[1],
        "xo_words": xop[0],
        "xo_scales": xop[1],
        "w_words": wp[0],
        "w_scales": wp[1],
        "wb_words": wbp[0],
        "wb_scales": wbp[1],
        "sx_words": sxp[0],
        "sx_scales": sxp[1],
        "ws_words": wsp[0],
        "ws_scales": wsp[1],
        "tz": (n((N, E))).astype(np.float32),
        "offs": striped(idx),
        "offs2": striped(idx2),
        "offs3": striped(idx3),
        "offs4": striped(idx4),
        "offs5": striped(idx5),
        "offs6": striped(idx6),
        "offs7": striped(idx7),
    }


def reference(xt_words, xt_scales, xo_words, xo_scales, w_words, w_scales, wb_words, wb_scales, sx_words, sx_scales, ws_words, ws_scales, tz, offs, offs2, offs3, offs4, offs5, offs6, offs7):
    idx = unstriped(offs)
    idx2 = unstriped(offs2)
    idx3 = unstriped(offs3)
    idx4 = unstriped(offs4)
    idx5 = unstriped(offs5)
    idx6 = unstriped(offs6)
    idx7 = unstriped(offs7)
    xtu = unpack_weight(xt_words, xt_scales, "e5m2")
    xou = unpack_weight(xo_words, xo_scales, "e4m3")
    wu = unpack_weight(w_words, w_scales, "e2m1")
    wbu = unpack_weight(wb_words, wb_scales, "e2m1")
    sxu = unpack_weight(sx_words, sx_scales, "e4m3")
    wsu = unpack_weight(ws_words, ws_scales, "e2m1")
    xtidxg = xtu[:, idx]
    a = wu.T @ xtidxg
    xoidx2g = xou[:, idx2]
    b = wu.T @ xoidx2g
    pw = np.zeros((R, C))
    pw[:, idx3] = a
    pv = np.zeros((R, C))
    pv[:, idx4] = b
    hid = np.abs(pw[:, idx5] - pv[:, idx6])
    hidq = mxq(hid, 0, "e4m3")
    p = wbu.T @ hidq + wsu.T @ sxu
    y = p + f64(tz)[:, idx7]
    return y

@@ -1,0 +1,216 @@
+import concourse.mybir as mybir
+
+F32 = mybir.dt.float32
+BF16 = mybir.dt.bfloat16
+I32 = mybir.dt.int32
+U32 = mybir.dt.uint32
+U16 = mybir.dt.uint16
+U8 = mybir.dt.uint8
+E4M3 = mybir.dt.float8_e4m3fn_x4
+E5M2 = mybir.dt.float8_e5m2_x4
+E2M1 = mybir.dt.float4_e2m1fn_x4
+ACT = mybir.ActivationFunctionType
+ALU = mybir.AluOpType
+
+P = 128
+PACK = 4
+T = 1024
+J = 256
+R = 512
+C = 512
+O = 256
+N = 256
+E = 1024
+HALF = O // 2
+FLOPS = 2 * (2 * 512 * R * J + 2 * 512 * N * O)
+
+
+def tile_list_oneforboth_twoboards_skip_tabled_kernel(
+    tc, xt_words, xt_scales, xo_words, xo_scales, w_words, w_scales, wb_words, wb_scales,
+    sx_words, sx_scales, ws_words, ws_scales, tz, offs, offs2, offs3, offs4, offs5, offs6, offs7, out,
+):
+    nc = tc.nc
+    with tc.tile_pool(name="sb", bufs=1) as sb, tc.psum_pool(name="ps", bufs=1) as ps:
+
+        def tile(name, shape, dtype, tag=None):
+            return sb.tile(shape, dtype, name=name, tag=tag or name, align_bytes=64)
+
+        def load_list(name, src):
+            t = tile(name, [P, J // 16], U16)
+            nc.sync.dma_start(t[:], src)
+            return t
+
+        def load_words(name, src, nbytes, dtype, queue):
+            t = tile(name, [P, nbytes // 4] if dtype == U32 else [P, nbytes], dtype)
+            queue.dma_start(t[:].bitcast(I32), src.bitcast(I32))
+            return t
+
+        def zeroed_plane(name, cols):
+            t = tile(name, [P, cols], U8)
+            nc.vector.memset(t[:].bitcast(I32), 0)
+            return t
+
+        def load_scale_rows(plane, src, quads, queue):
+            for q in quads:
+                queue.dma_start(plane[32 * q : 32 * q + 4, :].bitcast(I32), src[0, 4 * q : 4 * q + 4, :].bitcast(I32))
+
+        xt_sc = zeroed_plane("xt_sc", T)
+        w_sc_raw = zeroed_plane("w_sc_raw", R)
+        xo_sc = zeroed_plane("xo_sc", T)
+
+        l_xt = load_list("l_xt", offs)
+        w_raw = load_words("w_raw", w_words[0], 2 * R, U8, nc.sync)
+        xt_w = load_words("xt_w", xt_words[0].rearrange("p n t -> p (n t)"), 4 * T, U32, nc.sync)
+        load_scale_rows(xt_sc, xt_scales, range(4), nc.scalar)
+        load_scale_rows(w_sc_raw, w_scales, range(4), nc.sync)
+        l_xo = load_list("l_xo", offs2)
+        xo_w = load_words("xo_w", xo_words[0].rearrange("p n t -> p (n t)"), 4 * T, U32, nc.sync)
+        load_scale_rows(xo_sc, xo_scales, range(4), nc.sync)
+        l_pa = load_list("l_pa", offs3)
+        l_pb = load_list("l_pb", offs4)
+        l_ga = load_list("l_ga", offs5)
+        l_gb = load_list("l_gb", offs6)
+
+        small_sc = zeroed_plane("small_sc", 3 * N)
+        l_tz = load_list("l_tz", offs7)
+        tz_sb = [tile("tz%d" % n, [P, E], F32) for n in range(2)]
+        for n in range(2):
+            nc.sync.dma_start(tz_sb[n][:], tz[n * P : (n + 1) * P, :])
+        ws_w = load_words("ws_w", ws_words[0], 2 * N, U8, nc.sync)
+        sx_w = load_words("sx_w", sx_words[0].rearrange("p n t -> p (n t)"), 4 * O, U32, nc.sync)
+        wb_w = load_words("wb_w", wb_words[0], 2 * N, U8, nc.sync)
+        ws_sc, sx_sc, wb_sc = small_sc[:, 0:N], small_sc[:, N : 2 * N], small_sc[:, 2 * N : 3 * N]
+        load_scale_rows(ws_sc, ws_scales, range(4), nc.sync)
+        load_scale_rows(sx_sc, sx_scales, range(4), nc.sync)
+        load_scale_rows(wb_sc, wb_scales, range(4), nc.sync)
+
+        w_w = tile("w_w", [P, 2 * R], U8)
+        w_sc = tile("w_sc", [P, R], U8)
+        nc.vector.tensor_copy(
+            w_w[:].bitcast(U16).rearrange("p (t m) -> p t m", t=PACK),
+            w_raw[:].bitcast(U16).rearrange("p (m t) -> p t m", t=PACK),
+        )
+
+        def gather_packed(name, words, plane, lst):
+            gw = tile(name + "_w", [P, J], U32)
+            gs = tile(name + "_sc", [P, J], U8)
+            nc.vector.tensor_copy(gw[:], words[:].indirect(lst[:]))
+            nc.vector.tensor_copy(gs[:], plane[:].indirect(lst[:]))
+            return gw, gs
+
+        def first_product(dst, t, gw, gs, fmt):
+            nc.tensor.matmul_mx(
+                dst, lhsT=w_w[:, 2 * P * t : 2 * P * (t + 1)].bitcast(E2M1), lhsT_scale=w_sc[:, P * t : P * (t + 1)],
+                rhs=gw[:].bitcast(fmt), rhs_scale=gs[:], start=True, stop=True,
+            )
+
+        gxt_w, gxt_sc = gather_packed("gxt", xt_w, xt_sc, l_xt)
+        for u in range(2):
+            nc.vector.tensor_copy(
+                w_sc[:].rearrange("p (t m) -> p t m", t=PACK)[:, 2 * u : 2 * u + 2, :],
+                w_sc_raw[:].rearrange("p (m t) -> p t m", t=PACK)[:, 2 * u : 2 * u + 2, :],
+            )
+        gxo_w, gxo_sc = gather_packed("gxo", xo_w, xo_sc, l_xo)
+
+        boards_a = [tile("board_a%d" % t, [P, C], F32) for t in range(PACK)]
+        boards_b = [tile("board_b%d" % t, [P, C], F32) for t in range(PACK)]
+        for t in range(PACK):
+            nc.vector.memset(boards_a[t][:], 0.0)
+        for t in range(PACK):
+            nc.vector.memset(boards_b[t][:], 0.0)
+
+        pa0 = ps.tile([P, J], F32, name="pa0")
+        pa1 = ps.tile([P, J], F32, name="pa1")
+        pa23 = ps.tile([P, 2 * J], F32, name="pa23")
+        pb01 = ps.tile([P, 2 * J], F32, name="pb01")
+        pb23 = ps.tile([P, 2 * J], F32, name="pb23")
+        first_product(pa0[:], 0, gxt_w, gxt_sc, E5M2)
+        first_product(pa1[:], 1, gxt_w, gxt_sc, E5M2)
+        first_product(pa23[:, 0:J], 2, gxt_w, gxt_sc, E5M2)
+        first_product(pa23[:, J : 2 * J], 3, gxt_w, gxt_sc, E5M2)
+        first_product(pb01[:, 0:J], 0, gxo_w, gxo_sc, E4M3)
+        first_product(pb01[:, J : 2 * J], 1, gxo_w, gxo_sc, E4M3)
+        first_product(pb23[:, 0:J], 2, gxo_w, gxo_sc, E4M3)
+        first_product(pb23[:, J : 2 * J], 3, gxo_w, gxo_sc, E4M3)
+
+        a0 = tile("a0", [P, J], F32)
+        a1 = tile("a1", [P, J], F32)
+        a23 = tile("a23", [P, 2 * J], F32)
+        b01 = tile("b01", [P, 2 * J], F32)
+        b23 = tile("b23", [P, 2 * J], F32)
+        picked_a = [tile("picked_a%d" % t, [P, O], F32) for t in range(PACK)]
+        diff = tile("diff", [P, PACK, O], F32)
+
+        def scatter_s(board, lst, src):
+            nc.scalar.activation(board[:].indirect(lst[:]), src, ACT.Copy)
+
+        def scatter_v(board, lst, src):
+            nc.vector.tensor_copy(board[:].indirect(lst[:]), src)
+
+        def pick_a(t):
+            nc.scalar.activation(picked_a[t][:], boards_a[t][:].indirect(l_ga[:]), ACT.Copy)
+
+        def pick_b_sub(t, lo, hi):
+            nc.vector.tensor_tensor(
+                diff[:, t, lo:hi], boards_b[t][:].indirect(l_gb[:, lo // 16 : hi // 16]), picked_a[t][:, lo:hi], ALU.subtract
+            )
+
+        nc.scalar.activation(a0[:], pa0[:], ACT.Copy)
+        nc.scalar.activation(a1[:], pa1[:], ACT.Copy)
+        scatter_s(boards_a[0], l_pa, a0[:])
+        scatter_v(boards_a[1], l_pa, a1[:])
+        nc.scalar.activation(a23[:], pa23[:], ACT.Copy)
+        nc.vector.tensor_copy(b01[:], pb01[:])
+        pick_a(0)
+        scatter_v(boards_b[0], l_pb, b01[:, 0:J])
+        scatter_s(boards_a[2], l_pa, a23[:, 0:J])
+        pick_a(1)
+        scatter_v(boards_b[1], l_pb, b01[:, J : 2 * J])
+        nc.vector.tensor_copy(b23[:], pb23[:])
+        pick_b_sub(0, 0, O)
+        scatter_s(boards_a[3], l_pa, a23[:, J : 2 * J])
+        pick_a(2)
+        pick_a(3)
+        scatter_v(boards_b[2], l_pb, b23[:, 0:J])
+        pick_b_sub(1, 0, O)
+        scatter_s(boards_b[3], l_pb, b23[:, J : 2 * J])
+        pick_b_sub(2, 0, O)
+
+        tz_picked = tile("tz_picked", [P, 2, O], F32)
+        pp = [ps.tile([P, 2, HALF], F32, name="pp%d" % h) for h in range(2)]
+        for h in range(2):
+            for n in range(2):
+                nc.tensor.matmul_mx(
+                    pp[h][:, n, :], lhsT=ws_w[:, 2 * P * n : 2 * P * (n + 1)].bitcast(E2M1),
+                    lhsT_scale=ws_sc[:, P * n : P * (n + 1)],
+                    rhs=sx_w[:, HALF * h : HALF * (h + 1)].bitcast(E4M3), rhs_scale=sx_sc[:, HALF * h : HALF * (h + 1)],
+                    start=(n == 0), stop=False,
+                )
+        for h in range(2):
+            pick_b_sub(3, HALF * h, HALF * (h + 1))
+        nc.scalar.activation(tz_picked[:, 0, :], tz_sb[0][:].indirect(l_tz[:]), ACT.Copy)
+        nc.vector.tensor_copy(tz_picked[:, 1, :], tz_sb[1][:].indirect(l_tz[:]))
+        hid = [tile("hid0", [P, HALF * PACK], BF16, tag="tz0"), tile("hid1", [P, HALF * PACK], BF16)]
+        hid_w = [tile("hid_w0", [P, HALF], U32, tag="tz1"), tile("hid_w1", [P, HALF], U32)]
+        hid_sc = [tile("hid_sc%d" % h, [P, HALF], U8) for h in range(2)]
+        res = [tile("res%d" % h, [P, 2, HALF], F32) for h in range(2)]
+        for h in range(2):
+            nc.scalar.activation(
+                hid[h][:].rearrange("p (c i t) -> p c t i", i=4, t=PACK),
+                diff[:, :, HALF * h : HALF * (h + 1)].rearrange("p t (c i) -> p c t i", i=4),
+                ACT.Abs,
+            )
+        for h in range(2):
+            nc.vector.quantize_mx(hid_w[h][:].bitcast(E4M3), hid_sc[h][:], hid[h][:])
+            for n in range(2):
+                nc.tensor.matmul_mx(
+                    pp[h][:, n, :], lhsT=wb_w[:, 2 * P * n : 2 * P * (n + 1)].bitcast(E2M1),
+                    lhsT_scale=wb_sc[:, P * n : P * (n + 1)],
+                    rhs=hid_w[h][:].bitcast(E4M3), rhs_scale=hid_sc[h][:],
+                    start=False, stop=(n == 1),
+                )
+        for h in range(2):
+            nc.vector.tensor_tensor(res[h][:], pp[h][:], tz_picked[:, :, HALF * h : HALF * (h + 1)], ALU.add)
+            nc.sync.dma_start(
+                out[:, HALF * h : HALF * (h + 1)].rearrange("(n p) c -> p n c", p=P), res[h][:]
+            )

@@ -40,49 +40,38 @@ def tile_list_oneforboth_twoboards_skip_tabled_kernel(
             nc.sync.dma_start(t[:], src)
             return t
 
-        def load_words(name, src, nbytes, dtype, queue):
-            t = tile(name, [P, nbytes // 4] if dtype == U32 else [P, nbytes], dtype)
+        def load_words(name, src, nbytes, dtype, queue, tag=None):
+            t = tile(name, [P, nbytes // 4] if dtype == U32 else [P, nbytes], dtype, tag)
             queue.dma_start(t[:].bitcast(I32), src.bitcast(I32))
             return t
 
-        def zeroed_plane(name, cols):
+        def zeroed_plane(name, cols, engine):
             t = tile(name, [P, cols], U8)
-            nc.vector.memset(t[:].bitcast(I32), 0)
+            engine.memset(t[:].bitcast(I32), 0)
             return t
 
         def load_scale_rows(plane, src, quads, queue):
             for q in quads:
                 queue.dma_start(plane[32 * q : 32 * q + 4, :].bitcast(I32), src[0, 4 * q : 4 * q + 4, :].bitcast(I32))
 
-        xt_sc = zeroed_plane("xt_sc", T)
-        w_sc_raw = zeroed_plane("w_sc_raw", R)
-        xo_sc = zeroed_plane("xo_sc", T)
+        xt_sc = zeroed_plane("xt_sc", T, nc.vector)
+        w_sc_raw = zeroed_plane("w_sc_raw", R, nc.gpsimd)
+        xo_sc = zeroed_plane("xo_sc", T, nc.vector)
 
         l_xt = load_list("l_xt", offs)
         w_raw = load_words("w_raw", w_words[0], 2 * R, U8, nc.sync)
+        l_pa = load_list("l_pa", offs3)
+        load_scale_rows(xt_sc, xt_scales, range(4), nc.sync)
         xt_w = load_words("xt_w", xt_words[0].rearrange("p n t -> p (n t)"), 4 * T, U32, nc.sync)
-        load_scale_rows(xt_sc, xt_scales, range(4), nc.scalar)
         load_scale_rows(w_sc_raw, w_scales, range(4), nc.sync)
         l_xo = load_list("l_xo", offs2)
         xo_w = load_words("xo_w", xo_words[0].rearrange("p n t -> p (n t)"), 4 * T, U32, nc.sync)
         load_scale_rows(xo_sc, xo_scales, range(4), nc.sync)
-        l_pa = load_list("l_pa", offs3)
-        l_pb = load_list("l_pb", offs4)
         l_ga = load_list("l_ga", offs5)
+        l_pb = load_list("l_pb", offs4)
         l_gb = load_list("l_gb", offs6)
 
-        small_sc = zeroed_plane("small_sc", 3 * N)
         l_tz = load_list("l_tz", offs7)
-        tz_sb = [tile("tz%d" % n, [P, E], F32) for n in range(2)]
-        for n in range(2):
-            nc.sync.dma_start(tz_sb[n][:], tz[n * P : (n + 1) * P, :])
-        ws_w = load_words("ws_w", ws_words[0], 2 * N, U8, nc.sync)
-        sx_w = load_words("sx_w", sx_words[0].rearrange("p n t -> p (n t)"), 4 * O, U32, nc.sync)
-        wb_w = load_words("wb_w", wb_words[0], 2 * N, U8, nc.sync)
-        ws_sc, sx_sc, wb_sc = small_sc[:, 0:N], small_sc[:, N : 2 * N], small_sc[:, 2 * N : 3 * N]
-        load_scale_rows(ws_sc, ws_scales, range(4), nc.sync)
-        load_scale_rows(sx_sc, sx_scales, range(4), nc.sync)
-        load_scale_rows(wb_sc, wb_scales, range(4), nc.sync)
 
         w_w = tile("w_w", [P, 2 * R], U8)
         w_sc = tile("w_sc", [P, R], U8)
@@ -91,54 +80,40 @@ def tile_list_oneforboth_twoboards_skip_tabled_kernel(
             w_raw[:].bitcast(U16).rearrange("p (m t) -> p t m", t=PACK),
         )
 
-        def gather_packed(name, words, plane, lst):
-            gw = tile(name + "_w", [P, J], U32)
-            gs = tile(name + "_sc", [P, J], U8)
-            nc.vector.tensor_copy(gw[:], words[:].indirect(lst[:]))
-            nc.vector.tensor_copy(gs[:], plane[:].indirect(lst[:]))
-            return gw, gs
-
         def first_product(dst, t, gw, gs, fmt):
             nc.tensor.matmul_mx(
                 dst, lhsT=w_w[:, 2 * P * t : 2 * P * (t + 1)].bitcast(E2M1), lhsT_scale=w_sc[:, P * t : P * (t + 1)],
                 rhs=gw[:].bitcast(fmt), rhs_scale=gs[:], start=True, stop=True,
             )
 
-        gxt_w, gxt_sc = gather_packed("gxt", xt_w, xt_sc, l_xt)
+        gxt_w = tile("gxt_w", [P, J], U32)
+        gxt_sc = tile("gxt_sc", [P, J], U8)
+        nc.vector.tensor_copy(gxt_sc[:], xt_sc[:].indirect(l_xt[:]))
+        nc.vector.tensor_copy(gxt_w[:], xt_w[:].indirect(l_xt[:]))
         for u in range(2):
             nc.vector.tensor_copy(
                 w_sc[:].rearrange("p (t m) -> p t m", t=PACK)[:, 2 * u : 2 * u + 2, :],
                 w_sc_raw[:].rearrange("p (m t) -> p t m", t=PACK)[:, 2 * u : 2 * u + 2, :],
             )
-        gxo_w, gxo_sc = gather_packed("gxo", xo_w, xo_sc, l_xo)
 
         boards_a = [tile("board_a%d" % t, [P, C], F32) for t in range(PACK)]
         boards_b = [tile("board_b%d" % t, [P, C], F32) for t in range(PACK)]
-        for t in range(PACK):
-            nc.vector.memset(boards_a[t][:], 0.0)
-        for t in range(PACK):
-            nc.vector.memset(boards_b[t][:], 0.0)
+        for board in boards_a + boards_b:
+            nc.gpsimd.memset(board[:], 0.0)
+        small_sc = zeroed_plane("small_sc", 3 * N, nc.gpsimd)
 
-        pa0 = ps.tile([P, J], F32, name="pa0")
-        pa1 = ps.tile([P, J], F32, name="pa1")
-        pa23 = ps.tile([P, 2 * J], F32, name="pa23")
+        pa = [ps.tile([P, J], F32, name="pa%d" % t) for t in range(PACK)]
         pb01 = ps.tile([P, 2 * J], F32, name="pb01")
         pb23 = ps.tile([P, 2 * J], F32, name="pb23")
-        first_product(pa0[:], 0, gxt_w, gxt_sc, E5M2)
-        first_product(pa1[:], 1, gxt_w, gxt_sc, E5M2)
-        first_product(pa23[:, 0:J], 2, gxt_w, gxt_sc, E5M2)
-        first_product(pa23[:, J : 2 * J], 3, gxt_w, gxt_sc, E5M2)
-        first_product(pb01[:, 0:J], 0, gxo_w, gxo_sc, E4M3)
-        first_product(pb01[:, J : 2 * J], 1, gxo_w, gxo_sc, E4M3)
-        first_product(pb23[:, 0:J], 2, gxo_w, gxo_sc, E4M3)
-        first_product(pb23[:, J : 2 * J], 3, gxo_w, gxo_sc, E4M3)
+        for t in range(PACK):
+            first_product(pa[t][:], t, gxt_w, gxt_sc, E5M2)
 
         a0 = tile("a0", [P, J], F32)
         a1 = tile("a1", [P, J], F32)
-        a23 = tile("a23", [P, 2 * J], F32)
+        a2 = tile("a2", [P, J], F32)
         b01 = tile("b01", [P, 2 * J], F32)
         b23 = tile("b23", [P, 2 * J], F32)
-        picked_a = [tile("picked_a%d" % t, [P, O], F32) for t in range(PACK)]
+        picked_a = {}
         diff = tile("diff", [P, PACK, O], F32)
 
         def scatter_s(board, lst, src):
@@ -147,7 +122,8 @@ def tile_list_oneforboth_twoboards_skip_tabled_kernel(
         def scatter_v(board, lst, src):
             nc.vector.tensor_copy(board[:].indirect(lst[:]), src)
 
-        def pick_a(t):
+        def pick_a(t, tag=None):
+            picked_a[t] = tile("picked_a%d" % t, [P, O], F32, tag=tag)
             nc.scalar.activation(picked_a[t][:], boards_a[t][:].indirect(l_ga[:]), ACT.Copy)
 
         def pick_b_sub(t, lo, hi):
@@ -155,62 +131,77 @@ def tile_list_oneforboth_twoboards_skip_tabled_kernel(
                 diff[:, t, lo:hi], boards_b[t][:].indirect(l_gb[:, lo // 16 : hi // 16]), picked_a[t][:, lo:hi], ALU.subtract
             )
 
-        nc.scalar.activation(a0[:], pa0[:], ACT.Copy)
-        nc.scalar.activation(a1[:], pa1[:], ACT.Copy)
+        gxo_w = tile("gxo_w", [P, J], U32)
+        nc.vector.tensor_copy(gxo_w[:], xo_w[:].indirect(l_xo[:]))
+        nc.scalar.activation(a0[:], pa[0][:], ACT.Copy)
+        nc.vector.tensor_copy(a1[:], pa[1][:])
         scatter_s(boards_a[0], l_pa, a0[:])
         scatter_v(boards_a[1], l_pa, a1[:])
-        nc.scalar.activation(a23[:], pa23[:], ACT.Copy)
-        nc.vector.tensor_copy(b01[:], pb01[:])
+        gxo_sc = tile("gxo_sc", [P, J], U8, tag="a0")
+        nc.vector.tensor_copy(gxo_sc[:], xo_sc[:].indirect(l_xo[:]))
+        a3 = tile("a3", [P, J], F32, tag="xo_sc")
+        nc.vector.tensor_copy(a3[:], pa[3][:])
+        first_product(pb01[:, 0:J], 0, gxo_w, gxo_sc, E4M3)
+        first_product(pb01[:, J : 2 * J], 1, gxo_w, gxo_sc, E4M3)
+        first_product(pb23[:, 0:J], 2, gxo_w, gxo_sc, E4M3)
+        first_product(pb23[:, J : 2 * J], 3, gxo_w, gxo_sc, E4M3)
+        nc.scalar.activation(a2[:], pa[2][:], ACT.Copy)
         pick_a(0)
+        scatter_s(boards_a[2], l_pa, a2[:])
+        scatter_v(boards_a[3], l_pa, a3[:])
+        nc.scalar.activation(b01[:], pb01[:], ACT.Copy)
+        nc.scalar.activation(b23[:], pb23[:], ACT.Copy)
         scatter_v(boards_b[0], l_pb, b01[:, 0:J])
-        scatter_s(boards_a[2], l_pa, a23[:, 0:J])
-        pick_a(1)
-        scatter_v(boards_b[1], l_pb, b01[:, J : 2 * J])
-        nc.vector.tensor_copy(b23[:], pb23[:])
-        pick_b_sub(0, 0, O)
-        scatter_s(boards_a[3], l_pa, a23[:, J : 2 * J])
-        pick_a(2)
-        pick_a(3)
+        pick_a(1, "gxo_w")
+        scatter_s(boards_b[1], l_pb, b01[:, J : 2 * J])
         scatter_v(boards_b[2], l_pb, b23[:, 0:J])
-        pick_b_sub(1, 0, O)
+        pick_a(2, "a0")
+        pick_a(3, "w_w")
         scatter_s(boards_b[3], l_pb, b23[:, J : 2 * J])
-        pick_b_sub(2, 0, O)
+        for t in range(PACK - 1):
+            pick_b_sub(t, 0, O)
 
-        tz_picked = tile("tz_picked", [P, 2, O], F32)
-        pp = [ps.tile([P, 2, HALF], F32, name="pp%d" % h) for h in range(2)]
-        for h in range(2):
-            for n in range(2):
-                nc.tensor.matmul_mx(
-                    pp[h][:, n, :], lhsT=ws_w[:, 2 * P * n : 2 * P * (n + 1)].bitcast(E2M1),
-                    lhsT_scale=ws_sc[:, P * n : P * (n + 1)],
-                    rhs=sx_w[:, HALF * h : HALF * (h + 1)].bitcast(E4M3), rhs_scale=sx_sc[:, HALF * h : HALF * (h + 1)],
-                    start=(n == 0), stop=False,
-                )
-        for h in range(2):
-            pick_b_sub(3, HALF * h, HALF * (h + 1))
-        nc.scalar.activation(tz_picked[:, 0, :], tz_sb[0][:].indirect(l_tz[:]), ACT.Copy)
-        nc.vector.tensor_copy(tz_picked[:, 1, :], tz_sb[1][:].indirect(l_tz[:]))
-        hid = [tile("hid0", [P, HALF * PACK], BF16, tag="tz0"), tile("hid1", [P, HALF * PACK], BF16)]
-        hid_w = [tile("hid_w0", [P, HALF], U32, tag="tz1"), tile("hid_w1", [P, HALF], U32)]
-        hid_sc = [tile("hid_sc%d" % h, [P, HALF], U8) for h in range(2)]
-        res = [tile("res%d" % h, [P, 2, HALF], F32) for h in range(2)]
-        for h in range(2):
-            nc.scalar.activation(
-                hid[h][:].rearrange("p (c i t) -> p c t i", i=4, t=PACK),
-                diff[:, :, HALF * h : HALF * (h + 1)].rearrange("p t (c i) -> p c t i", i=4),
-                ACT.Abs,
+        ws_sc, sx_sc, wb_sc = small_sc[:, 0:N], small_sc[:, N : 2 * N], small_sc[:, 2 * N : 3 * N]
+        ws_w = load_words("ws_w", ws_words[0], 2 * N, U8, nc.sync, "w_raw")
+        sx_w = load_words("sx_w", sx_words[0].rearrange("p n t -> p (n t)"), 4 * O, U32, nc.sync, "xt_sc")
+        wb_w = load_words("wb_w", wb_words[0], 2 * N, U8, nc.sync, "w_sc_raw")
+        tz_sb = [tile("tz%d" % n, [P, E], F32, tag=("xt_w", "xo_w")[n]) for n in range(2)]
+        for n in range(2):
+            nc.sync.dma_start(tz_sb[n][:], tz[n * P : (n + 1) * P, :])
+        load_scale_rows(ws_sc, ws_scales, range(4), nc.sync)
+        load_scale_rows(sx_sc, sx_scales, range(4), nc.sync)
+        load_scale_rows(wb_sc, wb_scales, range(4), nc.sync)
+        pp = [ps.tile([P, O], F32, name="pp%d" % n, tag=("pb01", "pb23")[n]) for n in range(2)]
+        for n in range(2):
+            nc.tensor.matmul_mx(
+                pp[n][:], lhsT=ws_w[:, 2 * P * n : 2 * P * (n + 1)].bitcast(E2M1), lhsT_scale=ws_sc[:, P * n : P * (n + 1)],
+                rhs=sx_w[:].bitcast(E4M3), rhs_scale=sx_sc, start=True, stop=False,
             )
-        for h in range(2):
-            nc.vector.quantize_mx(hid_w[h][:].bitcast(E4M3), hid_sc[h][:], hid[h][:])
-            for n in range(2):
-                nc.tensor.matmul_mx(
-                    pp[h][:, n, :], lhsT=wb_w[:, 2 * P * n : 2 * P * (n + 1)].bitcast(E2M1),
-                    lhsT_scale=wb_sc[:, P * n : P * (n + 1)],
-                    rhs=hid_w[h][:].bitcast(E4M3), rhs_scale=hid_sc[h][:],
-                    start=False, stop=(n == 1),
-                )
-        for h in range(2):
-            nc.vector.tensor_tensor(res[h][:], pp[h][:], tz_picked[:, :, HALF * h : HALF * (h + 1)], ALU.add)
-            nc.sync.dma_start(
-                out[:, HALF * h : HALF * (h + 1)].rearrange("(n p) c -> p n c", p=P), res[h][:]
+        pick_b_sub(PACK - 1, 0, O)
+        tz_picked0 = tile("tz_picked0", [P, O], F32, tag="b23")
+        nc.scalar.activation(tz_picked0[:], tz_sb[0][:].indirect(l_tz[:]), ACT.Copy)
+        hid = tile("hid", [P, O * PACK], BF16, tag="xt_w")
+        hid_w = tile("hid_w", [P, O], U32)
+        hid_sc = tile("hid_sc", [P, O], U8)
+        nc.scalar.activation(
+            hid[:, 0 : HALF * PACK].rearrange("p (c i t) -> p c t i", i=4, t=PACK),
+            diff[:, :, 0:HALF].rearrange("p t (c i) -> p c t i", i=4),
+            ACT.Abs,
+        )
+        upper = diff[:, :, HALF:O].rearrange("p t c -> p c t")
+        nc.vector.scalar_tensor_tensor(
+            hid[:, HALF * PACK : O * PACK].rearrange("p (c t) -> p c t", t=PACK), upper, -1.0, upper, ALU.mult, ALU.max
+        )
+        tz_picked1 = tile("tz_picked1", [P, O], F32, tag="diff")
+        nc.scalar.activation(tz_picked1[:], tz_sb[1][:].indirect(l_tz[:]), ACT.Copy)
+        tz_picked = [tz_picked0, tz_picked1]
+        nc.vector.quantize_mx(hid_w[:].bitcast(E4M3), hid_sc[:], hid[:])
+        for n in range(2):
+            nc.tensor.matmul_mx(
+                pp[n][:], lhsT=wb_w[:, 2 * P * n : 2 * P * (n + 1)].bitcast(E2M1), lhsT_scale=wb_sc[:, P * n : P * (n + 1)],
+                rhs=hid_w[:].bitcast(E4M3), rhs_scale=hid_sc[:], start=False, stop=True,
             )
+        for n in range(2):
+            res = tile("res%d" % n, [P, O], F32)
+            nc.vector.tensor_tensor(res[:], pp[n][:], tz_picked[n][:], ALU.add)
+            nc.sync.dma_start(out[n * P : (n + 1) * P, :], res[:])

@@ -50,12 +50,17 @@ def tile_list_oneforboth_twoboards_skip_tabled_kernel(
             engine.memset(t[:].bitcast(I32), 0)
             return t
 
+        def zeroed_board(name, tag=None):
+            t = tile(name, [P, C], F32, tag)
+            nc.vector.memset(t[:], 0.0)
+            return t
+
         def load_scale_rows(plane, src, quads, queue):
             for q in quads:
                 queue.dma_start(plane[32 * q : 32 * q + 4, :].bitcast(I32), src[0, 4 * q : 4 * q + 4, :].bitcast(I32))
 
         xt_sc = zeroed_plane("xt_sc", T, nc.vector)
-        w_sc_raw = zeroed_plane("w_sc_raw", R, nc.gpsimd)
+        w_sc_raw = zeroed_plane("w_sc_raw", R, nc.vector)
         xo_sc = zeroed_plane("xo_sc", T, nc.vector)
 
         l_xt = load_list("l_xt", offs)
@@ -72,6 +77,10 @@ def tile_list_oneforboth_twoboards_skip_tabled_kernel(
         l_gb = load_list("l_gb", offs6)
 
         l_tz = load_list("l_tz", offs7)
+
+        boards_a = [zeroed_board("board_a%d" % t) for t in range(PACK)]
+        boards_b = [zeroed_board("board_b%d" % t) for t in range(2)]
+        small_sc = zeroed_plane("small_sc", 3 * N, nc.vector)
 
         w_w = tile("w_w", [P, 2 * R], U8)
         w_sc = tile("w_sc", [P, R], U8)
@@ -96,11 +105,7 @@ def tile_list_oneforboth_twoboards_skip_tabled_kernel(
                 w_sc_raw[:].rearrange("p (m t) -> p t m", t=PACK)[:, 2 * u : 2 * u + 2, :],
             )
 
-        boards_a = [tile("board_a%d" % t, [P, C], F32) for t in range(PACK)]
-        boards_b = [tile("board_b%d" % t, [P, C], F32) for t in range(PACK)]
-        for board in boards_a + boards_b:
-            nc.gpsimd.memset(board[:], 0.0)
-        small_sc = zeroed_plane("small_sc", 3 * N, nc.gpsimd)
+        boards_b.append(zeroed_board("board_b2", "w_sc_raw"))
 
         pa = [ps.tile([P, J], F32, name="pa%d" % t) for t in range(PACK)]
         pb01 = ps.tile([P, 2 * J], F32, name="pb01")
@@ -139,6 +144,7 @@ def tile_list_oneforboth_twoboards_skip_tabled_kernel(
         scatter_v(boards_a[1], l_pa, a1[:])
         gxo_sc = tile("gxo_sc", [P, J], U8, tag="a0")
         nc.vector.tensor_copy(gxo_sc[:], xo_sc[:].indirect(l_xo[:]))
+        boards_b.append(zeroed_board("board_b3", "a1"))
         a3 = tile("a3", [P, J], F32, tag="xo_sc")
         nc.vector.tensor_copy(a3[:], pa[3][:])
         first_product(pb01[:, 0:J], 0, gxo_w, gxo_sc, E4M3)
@@ -164,7 +170,7 @@ def tile_list_oneforboth_twoboards_skip_tabled_kernel(
         ws_sc, sx_sc, wb_sc = small_sc[:, 0:N], small_sc[:, N : 2 * N], small_sc[:, 2 * N : 3 * N]
         ws_w = load_words("ws_w", ws_words[0], 2 * N, U8, nc.sync, "w_raw")
         sx_w = load_words("sx_w", sx_words[0].rearrange("p n t -> p (n t)"), 4 * O, U32, nc.sync, "xt_sc")
-        wb_w = load_words("wb_w", wb_words[0], 2 * N, U8, nc.sync, "w_sc_raw")
+        wb_w = load_words("wb_w", wb_words[0], 2 * N, U8, nc.sync, "gxt_w")
         tz_sb = [tile("tz%d" % n, [P, E], F32, tag=("xt_w", "xo_w")[n]) for n in range(2)]
         for n in range(2):
             nc.sync.dma_start(tz_sb[n][:], tz[n * P : (n + 1) * P, :])

import concourse.mybir as mybir

F32 = mybir.dt.float32
BF16 = mybir.dt.bfloat16
I32 = mybir.dt.int32
U32 = mybir.dt.uint32
U16 = mybir.dt.uint16
U8 = mybir.dt.uint8
E4M3 = mybir.dt.float8_e4m3fn_x4
E5M2 = mybir.dt.float8_e5m2_x4
E2M1 = mybir.dt.float4_e2m1fn_x4
ACT = mybir.ActivationFunctionType
ALU = mybir.AluOpType

P = 128
PACK = 4
T = 1024
J = 256
R = 512
C = 512
O = 256
N = 256
E = 1024
HALF = O // 2
FLOPS = 2 * (2 * 512 * R * J + 2 * 512 * N * O)


def tile_list_oneforboth_twoboards_skip_tabled_kernel(
    tc, xt_words, xt_scales, xo_words, xo_scales, w_words, w_scales, wb_words, wb_scales,
    sx_words, sx_scales, ws_words, ws_scales, tz, offs, offs2, offs3, offs4, offs5, offs6, offs7, out,
):
    nc = tc.nc
    with tc.tile_pool(name="sb", bufs=1) as sb, tc.psum_pool(name="ps", bufs=1) as ps:

        def tile(name, shape, dtype, tag=None):
            return sb.tile(shape, dtype, name=name, tag=tag or name, align_bytes=64)

        def load_list(name, src):
            t = tile(name, [P, J // 16], U16)
            nc.sync.dma_start(t[:], src)
            return t

        def load_words(name, src, nbytes, dtype, queue, tag=None):
            t = tile(name, [P, nbytes // 4] if dtype == U32 else [P, nbytes], dtype, tag)
            queue.dma_start(t[:].bitcast(I32), src.bitcast(I32))
            return t

        def zeroed_plane(name, cols, engine):
            t = tile(name, [P, cols], U8)
            engine.memset(t[:].bitcast(I32), 0)
            return t

        def zeroed_board(name, tag=None):
            t = tile(name, [P, C], F32, tag)
            nc.vector.memset(t[:], 0.0)
            return t

        def load_scale_rows(plane, src, quads, queue):
            for q in quads:
                queue.dma_start(plane[32 * q : 32 * q + 4, :].bitcast(I32), src[0, 4 * q : 4 * q + 4, :].bitcast(I32))

        xt_sc = zeroed_plane("xt_sc", T, nc.vector)
        w_sc_raw = zeroed_plane("w_sc_raw", R, nc.vector)
        xo_sc = zeroed_plane("xo_sc", T, nc.vector)

        l_xt = load_list("l_xt", offs)
        w_raw = load_words("w_raw", w_words[0], 2 * R, U8, nc.sync)
        l_pa = load_list("l_pa", offs3)
        load_scale_rows(xt_sc, xt_scales, range(4), nc.sync)
        xt_w = load_words("xt_w", xt_words[0].rearrange("p n t -> p (n t)"), 4 * T, U32, nc.sync)
        load_scale_rows(w_sc_raw, w_scales, range(4), nc.sync)
        l_xo = load_list("l_xo", offs2)
        xo_w = load_words("xo_w", xo_words[0].rearrange("p n t -> p (n t)"), 4 * T, U32, nc.sync)
        load_scale_rows(xo_sc, xo_scales, range(4), nc.sync)
        l_ga = load_list("l_ga", offs5)
        l_pb = load_list("l_pb", offs4)
        l_gb = load_list("l_gb", offs6)

        l_tz = load_list("l_tz", offs7)

        boards_a = [zeroed_board("board_a%d" % t) for t in range(PACK)]
        boards_b = [zeroed_board("board_b%d" % t) for t in range(2)]
        small_sc = zeroed_plane("small_sc", 3 * N, nc.vector)

        w_w = tile("w_w", [P, 2 * R], U8)
        w_sc = tile("w_sc", [P, R], U8)
        nc.vector.tensor_copy(
            w_w[:].bitcast(U16).rearrange("p (t m) -> p t m", t=PACK),
            w_raw[:].bitcast(U16).rearrange("p (m t) -> p t m", t=PACK),
        )

        def first_product(dst, t, gw, gs, fmt):
            nc.tensor.matmul_mx(
                dst, lhsT=w_w[:, 2 * P * t : 2 * P * (t + 1)].bitcast(E2M1), lhsT_scale=w_sc[:, P * t : P * (t + 1)],
                rhs=gw[:].bitcast(fmt), rhs_scale=gs[:], start=True, stop=True,
            )

        gxt_w = tile("gxt_w", [P, J], U32)
        gxt_sc = tile("gxt_sc", [P, J], U8)
        nc.vector.tensor_copy(gxt_sc[:], xt_sc[:].indirect(l_xt[:]))
        nc.vector.tensor_copy(gxt_w[:], xt_w[:].indirect(l_xt[:]))
        for u in range(2):
            nc.vector.tensor_copy(
                w_sc[:].rearrange("p (t m) -> p t m", t=PACK)[:, 2 * u : 2 * u + 2, :],
                w_sc_raw[:].rearrange("p (m t) -> p t m", t=PACK)[:, 2 * u : 2 * u + 2, :],
            )

        boards_b.append(zeroed_board("board_b2", "w_sc_raw"))

        pa = [ps.tile([P, J], F32, name="pa%d" % t) for t in range(PACK)]
        pb01 = ps.tile([P, 2 * J], F32, name="pb01")
        pb23 = ps.tile([P, 2 * J], F32, name="pb23")
        for t in range(PACK):
            first_product(pa[t][:], t, gxt_w, gxt_sc, E5M2)

        a0 = tile("a0", [P, J], F32)
        a1 = tile("a1", [P, J], F32)
        a2 = tile("a2", [P, J], F32)
        b01 = tile("b01", [P, 2 * J], F32)
        b23 = tile("b23", [P, 2 * J], F32)
        picked_a = {}
        diff = tile("diff", [P, PACK, O], F32)

        def scatter_s(board, lst, src):
            nc.scalar.activation(board[:].indirect(lst[:]), src, ACT.Copy)

        def scatter_v(board, lst, src):
            nc.vector.tensor_copy(board[:].indirect(lst[:]), src)

        def pick_a(t, tag=None):
            picked_a[t] = tile("picked_a%d" % t, [P, O], F32, tag=tag)
            nc.scalar.activation(picked_a[t][:], boards_a[t][:].indirect(l_ga[:]), ACT.Copy)

        def pick_b_sub(t, lo, hi):
            nc.vector.tensor_tensor(
                diff[:, t, lo:hi], boards_b[t][:].indirect(l_gb[:, lo // 16 : hi // 16]), picked_a[t][:, lo:hi], ALU.subtract
            )

        gxo_w = tile("gxo_w", [P, J], U32)
        nc.vector.tensor_copy(gxo_w[:], xo_w[:].indirect(l_xo[:]))
        nc.scalar.activation(a0[:], pa[0][:], ACT.Copy)
        nc.vector.tensor_copy(a1[:], pa[1][:])
        scatter_s(boards_a[0], l_pa, a0[:])
        scatter_v(boards_a[1], l_pa, a1[:])
        gxo_sc = tile("gxo_sc", [P, J], U8, tag="a0")
        nc.vector.tensor_copy(gxo_sc[:], xo_sc[:].indirect(l_xo[:]))
        boards_b.append(zeroed_board("board_b3", "a1"))
        a3 = tile("a3", [P, J], F32, tag="xo_sc")
        nc.vector.tensor_copy(a3[:], pa[3][:])
        first_product(pb01[:, 0:J], 0, gxo_w, gxo_sc, E4M3)
        first_product(pb01[:, J : 2 * J], 1, gxo_w, gxo_sc, E4M3)
        first_product(pb23[:, 0:J], 2, gxo_w, gxo_sc, E4M3)
        first_product(pb23[:, J : 2 * J], 3, gxo_w, gxo_sc, E4M3)
        nc.scalar.activation(a2[:], pa[2][:], ACT.Copy)
        pick_a(0)
        scatter_s(boards_a[2], l_pa, a2[:])
        scatter_v(boards_a[3], l_pa, a3[:])
        nc.scalar.activation(b01[:], pb01[:], ACT.Copy)
        nc.scalar.activation(b23[:], pb23[:], ACT.Copy)
        scatter_v(boards_b[0], l_pb, b01[:, 0:J])
        pick_a(1, "gxo_w")
        scatter_s(boards_b[1], l_pb, b01[:, J : 2 * J])
        scatter_v(boards_b[2], l_pb, b23[:, 0:J])
        pick_a(2, "a0")
        pick_a(3, "w_w")
        scatter_s(boards_b[3], l_pb, b23[:, J : 2 * J])
        for t in range(PACK - 1):
            pick_b_sub(t, 0, O)

        ws_sc, sx_sc, wb_sc = small_sc[:, 0:N], small_sc[:, N : 2 * N], small_sc[:, 2 * N : 3 * N]
        ws_w = load_words("ws_w", ws_words[0], 2 * N, U8, nc.sync, "w_raw")
        sx_w = load_words("sx_w", sx_words[0].rearrange("p n t -> p (n t)"), 4 * O, U32, nc.sync, "xt_sc")
        wb_w = load_words("wb_w", wb_words[0], 2 * N, U8, nc.sync, "gxt_w")
        tz_sb = [tile("tz%d" % n, [P, E], F32, tag=("xt_w", "xo_w")[n]) for n in range(2)]
        for n in range(2):
            nc.sync.dma_start(tz_sb[n][:], tz[n * P : (n + 1) * P, :])
        load_scale_rows(ws_sc, ws_scales, range(4), nc.sync)
        load_scale_rows(sx_sc, sx_scales, range(4), nc.sync)
        load_scale_rows(wb_sc, wb_scales, range(4), nc.sync)
        pp = [ps.tile([P, O], F32, name="pp%d" % n, tag=("pb01", "pb23")[n]) for n in range(2)]
        for n in range(2):
            nc.tensor.matmul_mx(
                pp[n][:], lhsT=ws_w[:, 2 * P * n : 2 * P * (n + 1)].bitcast(E2M1), lhsT_scale=ws_sc[:, P * n : P * (n + 1)],
                rhs=sx_w[:].bitcast(E4M3), rhs_scale=sx_sc, start=True, stop=False,
            )
        pick_b_sub(PACK - 1, 0, O)
        tz_picked0 = tile("tz_picked0", [P, O], F32, tag="b23")
        nc.scalar.activation(tz_picked0[:], tz_sb[0][:].indirect(l_tz[:]), ACT.Copy)
        hid = tile("hid", [P, O * PACK], BF16, tag="xt_w")
        hid_w = tile("hid_w", [P, O], U32)
        hid_sc = tile("hid_sc", [P, O], U8)
        nc.scalar.activation(
            hid[:, 0 : HALF * PACK].rearrange("p (c i t) -> p c t i", i=4, t=PACK),
            diff[:, :, 0:HALF].rearrange("p t (c i) -> p c t i", i=4),
            ACT.Abs,
        )
        upper = diff[:, :, HALF:O].rearrange("p t c -> p c t")
        nc.vector.scalar_tensor_tensor(
            hid[:, HALF * PACK : O * PACK].rearrange("p (c t) -> p c t", t=PACK), upper, -1.0, upper, ALU.mult, ALU.max
        )
        tz_picked1 = tile("tz_picked1", [P, O], F32, tag="diff")
        nc.scalar.activation(tz_picked1[:], tz_sb[1][:].indirect(l_tz[:]), ACT.Copy)
        tz_picked = [tz_picked0, tz_picked1]
        nc.vector.quantize_mx(hid_w[:].bitcast(E4M3), hid_sc[:], hid[:])
        for n in range(2):
            nc.tensor.matmul_mx(
                pp[n][:], lhsT=wb_w[:, 2 * P * n : 2 * P * (n + 1)].bitcast(E2M1), lhsT_scale=wb_sc[:, P * n : P * (n + 1)],
                rhs=hid_w[:].bitcast(E4M3), rhs_scale=hid_sc[:], start=False, stop=True,
            )
        for n in range(2):
            res = tile("res%d" % n, [P, O], F32)
            nc.vector.tensor_tensor(res[:], pp[n][:], tz_picked[n][:], ALU.add)
            nc.sync.dma_start(out[n * P : (n + 1) * P, :], res[:])
